import numpy as np
import ml_dtypes


def mxq(x, axis, fmt="e4m3"):
    dtype, down = {"e4m3": (ml_dtypes.float8_e4m3fn, 7), "e5m2": (ml_dtypes.float8_e5m2, 14)}[fmt]
    v = np.moveaxis(np.asarray(x, np.float32).astype(ml_dtypes.bfloat16).astype(np.float64), axis, -1)
    blocks = v.reshape(v.shape[:-1] + (-1, 32))
    amax = np.abs(blocks).max(-1, keepdims=True)
    byte = np.maximum(np.where(amax > 0, np.frexp(amax)[1] - 1 + 127, 0) - down, 1)
    scale = np.exp2(byte - 127.0)
    codes = (blocks / scale).astype(np.float32).astype(dtype).astype(np.float64)
    return np.moveaxis((codes * scale).reshape(v.shape), -1, axis)


WIDE = False


def mx_kscale(k):
    if not WIDE:
        return np.ones(k)
    levels = np.array([10, -10, 5, -5, 0])
    if k % 512:
        return np.exp2(np.random.permutation(np.resize(levels, k // 32))).repeat(32)
    a = np.empty((k // 512, 16))
    for p in range(k // 512):
        a[p, :8] = np.random.permutation(np.resize(levels, 8))
        for g in range(8):
            far = levels[np.abs(levels - a[p, g]) >= 10]
            a[p, g + 8] = far[np.random.randint(len(far))]
    return np.exp2(a.ravel()).repeat(32)


def f64(x):
    return np.asarray(x).astype(np.float64)


def striped(idx):
    return np.tile(idx.reshape(-1, 16).T, (8, 1)).astype(np.uint16)


def unstriped(offs):
    return offs[:16].T.reshape(-1).astype(np.int64)


def striped8(idx):
    return np.concatenate([x.reshape(-1, 16).T for x in idx]).astype(np.uint16)


def runs(offs, k):
    lists = np.stack([offs[16 * r : 16 * r + 16].T.reshape(-1) for r in range(8)]).astype(np.int64)
    return lists[np.arange(k) % 512 // 64]


def pack_weight(w):
    k, n = w.shape
    w = f64(np.asarray(w, np.float32).astype(ml_dtypes.bfloat16)).reshape(k // 32, 32, n)
    amax = np.abs(w).max(1)
    byte = np.clip(np.where(amax > 0, np.frexp(amax)[1] - 1 + 127 - 7, 1), 1, 254)
    scaled = (w * np.exp2(127.0 - byte)[:, None, :]).reshape(k, n).astype(np.float32)
    words = np.ascontiguousarray(scaled.reshape(k // 512, 128, 4, n).transpose(0, 1, 3, 2)).astype(ml_dtypes.float8_e4m3fn).view(np.uint8)
    return words, np.ascontiguousarray(byte.astype(np.uint8).reshape(k // 512, 16, n))


def unpack_weight(words, scales):
    g, p, n, _ = words.shape
    vals = np.ascontiguousarray(words).view(ml_dtypes.float8_e4m3fn).astype(np.float64) * np.repeat(np.exp2(scales.astype(np.float64) - 127.0), 8, axis=1)[..., None]
    return vals.transpose(0, 1, 3, 2).reshape(g * 512, n)


def sigmoid(v):
    return 1.0 / (1.0 + np.exp(-np.maximum(v, -700.0)))

def planes(y):
    n, m = y.shape
    v = y.astype(np.float32).astype(ml_dtypes.bfloat16).astype(np.float64).reshape(n // 32, 32, m)
    top = np.abs(v).max(1)
    byte = np.clip(np.where(top > 0, np.frexp(top)[1] - 1 + 127 - 7, 1), 1, 254)
    codes = (v * np.exp2(127.0 - byte)[:, None, :]).reshape(n, m).astype(np.float32).astype(ml_dtypes.float8_e4m3fn).view(np.uint8)
    words = codes.reshape(n // 512, 128, 4, m).transpose(0, 1, 3, 2)
    return np.ascontiguousarray(words), np.ascontiguousarray(byte.astype(np.uint8).reshape(n // 512, 16, m))


K, T, S, N, H, W, C = 512, 2048, 512, 512, 512, 2048, 512


def setup_inputs():
    n = np.random.standard_normal
    s = mx_kscale(K)[:, None]
    u = mx_kscale(S)
    packed_xT = pack_weight(n((K, T)) * s)
    packed_w1 = pack_weight(n((K, H)) / np.sqrt(K) / s)
    packed_w2 = pack_weight(n((K, H)) / np.sqrt(K) / s)
    packed_w3 = pack_weight(n((H, N)) / np.sqrt(H) / u[:, None])
    return {
        "x_words": packed_xT[0],
        "x_scales": packed_xT[1],
        "w1_words": packed_w1[0],
        "w1_scales": packed_w1[1],
        "w2_words": packed_w2[0],
        "w2_scales": packed_w2[1],
        "tau": np.random.uniform(0.3, 0.9, (H, 1)).astype(np.float32),
        "gn": (np.random.uniform(0.5, 1.5, (H, 1)) * u[:, None]).astype(np.float32),
        "w3_words": packed_w3[0],
        "w3_scales": packed_w3[1],
        "gs": (np.random.uniform(0.5, 1.5, (K, 1)) / s).astype(np.float32),
        "sl": np.random.uniform(1.0, 2.0, (C, 1)).astype(np.float32),
        "th": (0.5 * n((C, 1))).astype(np.float32),
        "offs": striped(np.random.permutation(T)[:S]),
        "two": striped(np.random.permutation(T)[:S]),
        "n1": striped(np.random.randint(0, S, W)),
        "n2": striped(np.random.permutation(S)),
        "n3": striped(np.random.permutation(S)),
        "cand": striped(np.random.permutation(T)[:C]),
        "n4": striped8(np.stack([np.random.permutation(S) for _ in range(8)])),
        "n5": striped8(np.stack([np.random.permutation(S) for _ in range(8)])),
    }


def reference(x_words, x_scales, w1_words, w1_scales, w2_words, w2_scales, tau, gn, w3_words, w3_scales, gs, sl, th, offs, two, n1, n2, n3, cand, n4, n5):
    xq = unpack_weight(x_words, x_scales)[:, unstriped(offs)]
    y = unpack_weight(w1_words, w1_scales).T @ xq
    mb = y[:, unstriped(n1)]
    mx = mb.reshape(H, S, 4).max(axis=2)
    mn = mb.reshape(H, S, 4).min(axis=2)
    z = f64(gn) * (mx - (0.5 * mn))
    a = unpack_weight(w3_words, w3_scales).T @ mxq(z, 0, "e4m3")
    x_cand = unpack_weight(x_words, x_scales)[:, unstriped(cand)]
    x_two = unpack_weight(x_words, x_scales)[:, unstriped(two)]
    d = unpack_weight(w2_words, w2_scales).T @ x_two
    top = d.max(axis=1, keepdims=True)
    ea = np.exp(f64(tau) * (d[:, unstriped(n2)] - top))
    z2 = f64(gs) * (np.maximum(d, 2.0 * ea) - (0.5 * d[:, unstriped(n3)]))
    b = 0.0625 * ((x_cand.T @ mxq(z2, 0, "e4m3")))
    sg = sigmoid(f64(sl) * (b[np.arange(C)[:, None], runs(n4, C)] - f64(th)))
    out_0 = np.maximum(a * sg, b[np.arange(C)[:, None], runs(n5, C)] - b)
    return (out_0,) + planes(out_0)

@@ -1,0 +1,249 @@
+from contextlib import ExitStack
+
+import concourse.mybir as mybir
+
+F32 = mybir.dt.float32
+BF16 = mybir.dt.bfloat16
+I32 = mybir.dt.int32
+U32 = mybir.dt.uint32
+U16 = mybir.dt.uint16
+U8 = mybir.dt.uint8
+FP8X4 = mybir.dt.float8_e4m3fn_x4
+ALU = mybir.AluOpType
+ACT = mybir.ActivationFunctionType
+
+P = 128
+PACK = 4
+T = 2048
+S = 512
+MEMBERS = 4
+CHUNK = 128
+CHUNKS = S // CHUNK
+HALF = S // 2
+SPARE = 32
+PER_COL = 16
+FLOPS = 4 * 2 * 512 * 512 * 512
+
+
+def tile_picked_tfcdmxbgspanecl_none_po_kernel(
+    tc, x_words, x_scales, w1_words, w1_scales, w2_words, w2_scales, tau, gn, w3_words, w3_scales,
+    gs, sl, th, offs, two, n1, n2, n3, cand, n4, n5, out_0, out_1, out_2,
+):
+    nc = tc.nc
+    with ExitStack() as ctx:
+        keep = ctx.enter_context(tc.tile_pool(name="keep", bufs=1))
+        work = ctx.enter_context(tc.tile_pool(name="work", bufs=2))
+        psum = ctx.enter_context(tc.psum_pool(name="psum", bufs=1))
+
+        def sb(name, shape, dtype):
+            return keep.tile(shape, dtype, name=name, align_bytes=64)
+
+        def ring(tag, shape, dtype, bufs):
+            return work.tile(shape, dtype, name=tag, tag=tag, bufs=bufs, align_bytes=64)
+
+        def load_list(name, src):
+            tile = keep.tile(list(src.shape), U16, name=name)
+            nc.sync.dma_start(tile[:], src)
+            return tile
+
+        def load_words(name, src, width):
+            tile = sb(name, [P, width], U32)
+            nc.sync.dma_start(tile[:].bitcast(I32), src[0].rearrange("p n t -> p (n t)").bitcast(I32))
+            return tile
+
+        def load_scale_rows(queue, tile, src, first):
+            for q in range(4):
+                queue.dma_start(
+                    tile[32 * q + first : 32 * q + first + 4, :].bitcast(I32),
+                    src[0, 4 * q : 4 * q + 4, :].bitcast(I32),
+                )
+
+        def load_rows(name, src):
+            tile = sb(name, [P, PACK], F32)
+            nc.sync.dma_start(tile[:], src.rearrange("(p t) o -> p (t o)", t=PACK))
+            return tile
+
+        def deal(copy, name, src, dtype, run):
+            dst = sb(name, [P, S], dtype)
+            copy(
+                dst[:].rearrange("p (t m i) -> p m t i", t=PACK, i=run),
+                src[:].rearrange("p (m i t) -> p m t i", t=PACK, i=run),
+            )
+            return dst
+
+        def pick(name, lst):
+            words = sb(name + "_words", [P, S], U32)
+            scales = sb(name + "_scales", [P, S], U8)
+            nc.vector.tensor_copy(words[:], xw[:].indirect(lst[:]))
+            nc.vector.tensor_copy(scales[:], xs[:].indirect(lst[:]))
+            return words, scales
+
+        def product(out, lhs_words, lhs_scales, first, t, rhs_words, rhs_scales):
+            cols = slice(t * P, (t + 1) * P)
+            nc.tensor.matmul_mx(
+                out=out, lhsT=lhs_words[:, cols].bitcast(FP8X4), lhsT_scale=lhs_scales[first:P, cols],
+                rhs=rhs_words.bitcast(FP8X4), rhs_scale=rhs_scales, start=True, stop=True,
+            )
+
+        def quantise(name, planes, width, words, scales):
+            woven = sb(name, [P, width, PACK], BF16)
+            nc.vector.tensor_copy(woven[:], planes.rearrange("p t j -> p j t"))
+            nc.vector.quantize_mx(out=words.bitcast(FP8X4), scales=scales, in_=woven[:].rearrange("p j t -> p (j t)"))
+
+        banks = [psum.tile([P, S], F32, name=f"bank{i}") for i in range(8)]
+
+        xs = sb("xs", [P, T], U8)
+        w1s_raw = sb("w1s_raw", [P, S], U8)
+        w23s_raw = sb("w23s_raw", [P, S], U8)
+        nc.vector.memset(xs[:].bitcast(I32), 0)
+        nc.gpsimd.memset(w1s_raw[:].bitcast(I32), 0)
+        nc.gpsimd.memset(w23s_raw[:].bitcast(I32), 0)
+        y = [sb(f"y{t}", [P, S + SPARE], F32) for t in range(PACK)]
+        for t in range(PACK):
+            nc.gpsimd.memset(y[t][:, S:], 0.0)
+
+        offs_l = load_list("offs_l", offs)
+        xw = load_words("xw", x_words, T)
+        load_scale_rows(nc.sync, xs, x_scales, 0)
+        load_scale_rows(nc.sync, w1s_raw, w1_scales, 0)
+        w1w_raw = load_words("w1w_raw", w1_words, S)
+        two_l = load_list("two_l", two)
+        n1_l = load_list("n1_l", n1)
+        cand_l = load_list("cand_l", cand)
+        w2w_raw = load_words("w2w_raw", w2_words, S)
+        load_scale_rows(nc.sync, w23s_raw, w2_scales, 0)
+        load_scale_rows(nc.sync, w23s_raw, w3_scales, 4)
+        tau_t = load_rows("tau_t", tau)
+        gn_t = load_rows("gn_t", gn)
+        n2_l = load_list("n2_l", n2)
+        w3w_raw = load_words("w3w_raw", w3_words, S)
+        n3_l = load_list("n3_l", n3)
+        gs_t = load_rows("gs_t", gs)
+        n4_l = load_list("n4_l", n4)
+        n5_l = load_list("n5_l", n5)
+        sl_t = load_rows("sl_t", sl)
+        th_t = load_rows("th_t", th)
+
+        w1s = deal(nc.vector.tensor_copy, "w1s", w1s_raw, U8, 16)
+        w1w = deal(nc.scalar.copy, "w1w", w1w_raw, U32, 4)
+        w2w = deal(nc.scalar.copy, "w2w", w2w_raw, U32, 4)
+        xo_w, xo_s = pick("xo", offs_l)
+        for t in range(PACK):
+            product(banks[t][:], w1w, w1s, 0, t, xo_w[:], xo_s[:])
+            nc.scalar.copy(y[t][:, :S], banks[t][:])
+
+        xt_w, xt_s = pick("xt", two_l)
+        w23s = deal(nc.vector.tensor_copy, "w23s", w23s_raw, U8, 16)
+        d = [sb(f"d{t}", [P, S], F32) for t in range(PACK)]
+        top = sb("top", [P, PACK], F32)
+        for t in range(PACK):
+            product(banks[4 + t][:], w2w, w23s, 0, t, xt_w[:], xt_s[:])
+            nc.vector.tensor_scalar(d[t][:], banks[4 + t][:], 1.0, None, ALU.mult, ALU.max, accum_out=top[:, t : t + 1])
+        exp_bias = sb("exp_bias", [P, PACK], F32)
+        nc.vector.scalar_tensor_tensor(exp_bias[:], top[:], -1.0, tau_t[:], ALU.mult, ALU.mult)
+
+        w3w = deal(nc.scalar.copy, "w3w", w3w_raw, U32, 4)
+
+        def members(c):
+            entries = CHUNK * MEMBERS
+            lst = n1_l[:, c * entries // PER_COL : (c + 1) * entries // PER_COL]
+            z = sb(f"z{c}", [P, PACK, CHUNK], BF16)
+            for u in range(2):
+                mb = ring("mb", [P, 2, entries], F32, 4)
+                for k in range(2):
+                    nc.scalar.activation(mb[:, k, :], y[2 * u + k][:].indirect(lst), ACT.Copy)
+                four = mb[:].rearrange("p k (j e) -> p (k j) e", e=MEMBERS)
+                hi = ring("hi", [P, 2 * CHUNK, 2], F32, 2)
+                lo = ring("lo", [P, 2 * CHUNK, 2], F32, 2)
+                nc.vector.tensor_tensor(hi[:], four[:, :, 0:2], four[:, :, 2:4], ALU.max)
+                nc.vector.tensor_tensor(lo[:], four[:, :, 0:2], four[:, :, 2:4], ALU.min)
+                mx = ring("mx", [P, 2 * CHUNK], F32, 2)
+                mn = ring("mn", [P, 2 * CHUNK], F32, 2)
+                nc.vector.tensor_tensor(mx[:], hi[:, :, 0], hi[:, :, 1], ALU.max)
+                nc.vector.tensor_tensor(mn[:], lo[:, :, 0], lo[:, :, 1], ALU.min)
+                spread = ring("spread", [P, 2 * CHUNK], F32, 2)
+                nc.vector.scalar_tensor_tensor(spread[:], mn[:], -0.5, mx[:], ALU.mult, ALU.add)
+                for k in range(2):
+                    t = 2 * u + k
+                    nc.vector.tensor_scalar(z[:, t, :], spread[:, k * CHUNK : (k + 1) * CHUNK], gn_t[:, t : t + 1], None, ALU.mult)
+            zw = sb(f"zw{c}", [P, CHUNK], U32)
+            zs = sb(f"zs{c}", [P, CHUNK], U8)
+            quantise(f"zq{c}", z[:], CHUNK, zw[:], zs[:])
+            for t in range(PACK):
+                product(banks[4 + c][:, t * CHUNK : (t + 1) * CHUNK], w3w, w23s, 4, t, zw[:], zs[:])
+
+        def halves(lst):
+            return [(slice(h * HALF, (h + 1) * HALF), lst[:, h * HALF // PER_COL : (h + 1) * HALF // PER_COL]) for h in range(2)]
+
+        members(0)
+
+        xc_w0, xc_s0 = pick("xc", cand_l)
+        xc_w = deal(nc.vector.tensor_copy, "xc_w", xc_w0, U32, 4)
+        xc_s = deal(nc.vector.tensor_copy, "xc_s", xc_s0, U8, 16)
+        larger = []
+        for t in range(PACK):
+            ea = sb(f"ea{t}", [P, S], F32)
+            for cols, lst in halves(n2_l):
+                nc.scalar.activation(ea[:, cols], d[t][:].indirect(lst), ACT.Exp, bias=exp_bias[:, t : t + 1], scale=tau_t[:, t : t + 1])
+            big = sb(f"larger{t}", [P, S], F32)
+            nc.vector.scalar_tensor_tensor(big[:], ea[:], 2.0, d[t][:], ALU.mult, ALU.max)
+            larger.append(big)
+
+        members(1)
+
+        z2 = sb("z2", [P, PACK, S], BF16)
+        for t in range(PACK):
+            d3 = sb(f"d3_{t}", [P, S], F32)
+            for cols, lst in halves(n3_l):
+                nc.scalar.activation(d3[:, cols], d[t][:].indirect(lst), ACT.Copy)
+            diff = ring("diff", [P, S], F32, 2)
+            nc.vector.scalar_tensor_tensor(diff[:], d3[:], -0.5, larger[t][:], ALU.mult, ALU.add)
+            nc.vector.tensor_scalar(z2[:, t, :], diff[:], gs_t[:, t : t + 1], None, ALU.mult)
+        z2w = sb("z2w", [P, S], U32)
+        z2s = sb("z2s", [P, S], U8)
+        quantise("z2q", z2[:], S, z2w[:], z2s[:])
+
+        members(2)
+
+        sig_bias = sb("sig_bias", [P, PACK], F32)
+        nc.vector.scalar_tensor_tensor(sig_bias[:], sl_t[:], -1.0, th_t[:], ALU.mult, ALU.mult)
+        b = [sb(f"b{t}", [P, S], F32) for t in range(PACK)]
+        b_again = [sb(f"b_again{t}", [P, S], F32) for t in range(PACK)]
+        for t in range(PACK):
+            product(banks[t][:], xc_w, xc_s, 0, t, z2w[:], z2s[:])
+            nc.scalar.activation(b[t][:], banks[t][:], ACT.Copy, scale=0.0625)
+            nc.sync.dma_start(b_again[t][:], b[t][:])
+        sg = [sb(f"sg{h}", [P, PACK, HALF], F32) for h in range(2)]
+        step = [sb(f"step{h}", [P, PACK, HALF], F32) for h in range(2)]
+        for h, (cols, lst) in enumerate(halves(n4_l)):
+            for t in range(PACK):
+                nc.scalar.activation(sg[h][:, t, :], b[t][:].indirect(lst), ACT.Sigmoid, bias=sig_bias[:, t : t + 1], scale=sl_t[:, t : t + 1])
+        for h, (cols, lst) in enumerate(halves(n5_l)):
+            for t in range(PACK):
+                nc.vector.tensor_tensor(step[h][:, t, :], b[t][:].indirect(lst), b_again[t][:, cols], ALU.subtract)
+
+        ow = sb("ow", [P, S], U32)
+        osc = sb("osc", [P, S], U8)
+        out_rows = out_0.rearrange("(p t) j -> p t j", t=PACK)
+        out_words = out_1[0].rearrange("p n t -> p (n t)").bitcast(I32)
+
+        def finish(c):
+            cols = slice(c * CHUNK, (c + 1) * CHUNK)
+            h, part = divmod(c, 2)
+            part_cols = slice(part * CHUNK, (part + 1) * CHUNK)
+            gated = ring("gated", [P, PACK, CHUNK], F32, 2)
+            nc.vector.tensor_tensor(gated[:], banks[4 + c][:].rearrange("p (t j) -> p t j", t=PACK), sg[h][:, :, part_cols], ALU.mult)
+            res = sb(f"res{c}", [P, PACK, CHUNK], F32)
+            nc.vector.tensor_tensor(res[:], gated[:], step[h][:, :, part_cols], ALU.max)
+            nc.sync.dma_start(out_rows[:, :, cols], res[:])
+            quantise(f"oq{c}", res[:], CHUNK, ow[:, cols], osc[:, cols])
+            nc.sync.dma_start(out_words[:, cols], ow[:, cols].bitcast(I32))
+
+        finish(0)
+        finish(1)
+        members(3)
+        finish(2)
+        finish(3)
+        for q in range(4):
+            queue = nc.scalar if q % 2 else nc.sync
+            queue.dma_start(out_2[0, 4 * q : 4 * q + 4, :].bitcast(I32), osc[32 * q : 32 * q + 4, :].bitcast(I32))

@@ -41,6 +41,9 @@ def tile_picked_tfcdmxbgspanecl_none_po_kernel(
         def ring(tag, shape, dtype, bufs):
             return work.tile(shape, dtype, name=tag, tag=tag, bufs=bufs, align_bytes=64)
 
+        def reuse(tag, name, shape, dtype):
+            return work.tile(shape, dtype, name=name, tag=tag, bufs=1, align_bytes=64)
+
         def load_list(name, src):
             tile = keep.tile(list(src.shape), U16, name=name)
             nc.sync.dma_start(tile[:], src)
@@ -59,7 +62,7 @@ def tile_picked_tfcdmxbgspanecl_none_po_kernel(
                 )
 
         def load_rows(name, src):
-            tile = sb(name, [P, PACK], F32)
+            tile = reuse(name, name, [P, PACK], F32)
             nc.sync.dma_start(tile[:], src.rearrange("(p t) o -> p (t o)", t=PACK))
             return tile
 
@@ -71,9 +74,10 @@ def tile_picked_tfcdmxbgspanecl_none_po_kernel(
             )
             return dst
 
-        def pick(name, lst):
-            words = sb(name + "_words", [P, S], U32)
-            scales = sb(name + "_scales", [P, S], U8)
+        def pick(name, lst, tags=None):
+            tags = tags or (name + "_words", name + "_scales")
+            words = reuse(tags[0], name + "_words", [P, S], U32)
+            scales = reuse(tags[1], name + "_scales", [P, S], U8)
             nc.vector.tensor_copy(words[:], xw[:].indirect(lst[:]))
             nc.vector.tensor_copy(scales[:], xs[:].indirect(lst[:]))
             return words, scales
@@ -102,20 +106,20 @@ def tile_picked_tfcdmxbgspanecl_none_po_kernel(
         for t in range(PACK):
             nc.gpsimd.memset(y[t][:, S:], 0.0)
 
-        offs_l = load_list("offs_l", offs)
         xw = load_words("xw", x_words, T)
+        w1w_raw = load_words("w1w_raw", w1_words, S)
+        offs_l = load_list("offs_l", offs)
         load_scale_rows(nc.sync, xs, x_scales, 0)
         load_scale_rows(nc.sync, w1s_raw, w1_scales, 0)
-        w1w_raw = load_words("w1w_raw", w1_words, S)
         two_l = load_list("two_l", two)
         n1_l = load_list("n1_l", n1)
-        cand_l = load_list("cand_l", cand)
         w2w_raw = load_words("w2w_raw", w2_words, S)
         load_scale_rows(nc.sync, w23s_raw, w2_scales, 0)
         load_scale_rows(nc.sync, w23s_raw, w3_scales, 4)
         tau_t = load_rows("tau_t", tau)
-        gn_t = load_rows("gn_t", gn)
         n2_l = load_list("n2_l", n2)
+        cand_l = load_list("cand_l", cand)
+        gn_t = load_rows("gn_t", gn)
         w3w_raw = load_words("w3w_raw", w3_words, S)
         n3_l = load_list("n3_l", n3)
         gs_t = load_rows("gs_t", gs)
@@ -123,6 +127,17 @@ def tile_picked_tfcdmxbgspanecl_none_po_kernel(
         n5_l = load_list("n5_l", n5)
         sl_t = load_rows("sl_t", sl)
         th_t = load_rows("th_t", th)
+
+        def halves(lst):
+            return [(slice(h * HALF, (h + 1) * HALF), lst[:, h * HALF // PER_COL : (h + 1) * HALF // PER_COL]) for h in range(2)]
+
+        def quantise_scaled(name, planes, gain, width, words, scales):
+            woven = reuse(name, name, [P, width, PACK], BF16)
+            scaled = reuse(name + "_planes", name + "_planes", [P, PACK, width], BF16)
+            for t in range(PACK):
+                nc.vector.tensor_scalar(scaled[:, t, :], planes[:, t, :], gain[:, t : t + 1], None, ALU.mult)
+            nc.vector.tensor_copy(woven[:], scaled[:].rearrange("p t j -> p j t"))
+            nc.vector.quantize_mx(out=words.bitcast(FP8X4), scales=scales, in_=woven[:].rearrange("p j t -> p (j t)"))
 
         w1s = deal(nc.vector.tensor_copy, "w1s", w1s_raw, U8, 16)
         w1w = deal(nc.scalar.copy, "w1w", w1w_raw, U32, 4)
@@ -135,99 +150,107 @@ def tile_picked_tfcdmxbgspanecl_none_po_kernel(
         xt_w, xt_s = pick("xt", two_l)
         w23s = deal(nc.vector.tensor_copy, "w23s", w23s_raw, U8, 16)
         d = [sb(f"d{t}", [P, S], F32) for t in range(PACK)]
-        top = sb("top", [P, PACK], F32)
+        top = reuse("top", "top", [P, PACK], F32)
+        exp_bias = sb("exp_bias", [P, PACK], F32)
         for t in range(PACK):
             product(banks[4 + t][:], w2w, w23s, 0, t, xt_w[:], xt_s[:])
             nc.vector.tensor_scalar(d[t][:], banks[4 + t][:], 1.0, None, ALU.mult, ALU.max, accum_out=top[:, t : t + 1])
-        exp_bias = sb("exp_bias", [P, PACK], F32)
         nc.vector.scalar_tensor_tensor(exp_bias[:], top[:], -1.0, tau_t[:], ALU.mult, ALU.mult)
 
-        w3w = deal(nc.scalar.copy, "w3w", w3w_raw, U32, 4)
+        entries = CHUNK * MEMBERS
 
-        def members(c):
-            entries = CHUNK * MEMBERS
+        def fetch(c):
             lst = n1_l[:, c * entries // PER_COL : (c + 1) * entries // PER_COL]
-            z = sb(f"z{c}", [P, PACK, CHUNK], BF16)
-            for u in range(2):
-                mb = ring("mb", [P, 2, entries], F32, 4)
-                for k in range(2):
-                    nc.scalar.activation(mb[:, k, :], y[2 * u + k][:].indirect(lst), ACT.Copy)
-                four = mb[:].rearrange("p k (j e) -> p (k j) e", e=MEMBERS)
-                hi = ring("hi", [P, 2 * CHUNK, 2], F32, 2)
-                lo = ring("lo", [P, 2 * CHUNK, 2], F32, 2)
-                nc.vector.tensor_tensor(hi[:], four[:, :, 0:2], four[:, :, 2:4], ALU.max)
-                nc.vector.tensor_tensor(lo[:], four[:, :, 0:2], four[:, :, 2:4], ALU.min)
-                mx = ring("mx", [P, 2 * CHUNK], F32, 2)
-                mn = ring("mn", [P, 2 * CHUNK], F32, 2)
-                nc.vector.tensor_tensor(mx[:], hi[:, :, 0], hi[:, :, 1], ALU.max)
-                nc.vector.tensor_tensor(mn[:], lo[:, :, 0], lo[:, :, 1], ALU.min)
-                spread = ring("spread", [P, 2 * CHUNK], F32, 2)
-                nc.vector.scalar_tensor_tensor(spread[:], mn[:], -0.5, mx[:], ALU.mult, ALU.add)
-                for k in range(2):
-                    t = 2 * u + k
-                    nc.vector.tensor_scalar(z[:, t, :], spread[:, k * CHUNK : (k + 1) * CHUNK], gn_t[:, t : t + 1], None, ALU.mult)
+            mb = reuse(("mbA", "xc_scales", "mbA", "z2q")[c], f"mb{c}", [P, PACK, entries], F32)
+            for t in range(PACK):
+                if (c, t) in ((1, 0),):
+                    nc.vector.tensor_copy(mb[:, t, :], y[t][:].indirect(lst))
+                else:
+                    nc.scalar.activation(mb[:, t, :], y[t][:].indirect(lst), ACT.Copy)
+            return mb
+
+        def members(c, mb):
+            four = mb[:].rearrange("p t (j e) -> p (t j) e", e=MEMBERS)
+            pairs = reuse(("top", "z2q_planes", "z2q_planes", "z2q_planes")[c], f"pairs{c}", [P, 2, PACK * CHUNK, 2], F32)
+            hi, lo = pairs[:, 0], pairs[:, 1]
+            nc.vector.tensor_tensor(hi, four[:, :, 0:2], four[:, :, 2:4], ALU.max)
+            nc.vector.tensor_tensor(lo, four[:, :, 0:2], four[:, :, 2:4], ALU.min)
+            mx = reuse("mx", f"mx{c}", [P, PACK * CHUNK], F32)
+            mn = reuse("mn", f"mn{c}", [P, PACK * CHUNK], F32)
+            nc.vector.tensor_tensor(mx[:], hi[:, :, 0], hi[:, :, 1], ALU.max)
+            nc.vector.tensor_tensor(mn[:], lo[:, :, 0], lo[:, :, 1], ALU.min)
+            spread = ring("spread", [P, PACK, CHUNK], F32, 2)
+            nc.vector.scalar_tensor_tensor(spread[:].rearrange("p t j -> p (t j)"), mn[:], -0.5, mx[:], ALU.mult, ALU.add)
             zw = sb(f"zw{c}", [P, CHUNK], U32)
             zs = sb(f"zs{c}", [P, CHUNK], U8)
-            quantise(f"zq{c}", z[:], CHUNK, zw[:], zs[:])
+            quantise_scaled(f"zq{c}", spread[:], gn_t, CHUNK, zw[:], zs[:])
+            return zw, zs
+
+        def mix(c, zw, zs):
             for t in range(PACK):
                 product(banks[4 + c][:, t * CHUNK : (t + 1) * CHUNK], w3w, w23s, 4, t, zw[:], zs[:])
 
-        def halves(lst):
-            return [(slice(h * HALF, (h + 1) * HALF), lst[:, h * HALF // PER_COL : (h + 1) * HALF // PER_COL]) for h in range(2)]
-
-        members(0)
-
-        xc_w0, xc_s0 = pick("xc", cand_l)
-        xc_w = deal(nc.vector.tensor_copy, "xc_w", xc_w0, U32, 4)
-        xc_s = deal(nc.vector.tensor_copy, "xc_s", xc_s0, U8, 16)
-        larger = []
-        for t in range(PACK):
-            ea = sb(f"ea{t}", [P, S], F32)
-            for cols, lst in halves(n2_l):
-                nc.scalar.activation(ea[:, cols], d[t][:].indirect(lst), ACT.Exp, bias=exp_bias[:, t : t + 1], scale=tau_t[:, t : t + 1])
-            big = sb(f"larger{t}", [P, S], F32)
-            nc.vector.scalar_tensor_tensor(big[:], ea[:], 2.0, d[t][:], ALU.mult, ALU.max)
-            larger.append(big)
-
-        members(1)
-
-        z2 = sb("z2", [P, PACK, S], BF16)
-        for t in range(PACK):
-            d3 = sb(f"d3_{t}", [P, S], F32)
-            for cols, lst in halves(n3_l):
-                nc.scalar.activation(d3[:, cols], d[t][:].indirect(lst), ACT.Copy)
-            diff = ring("diff", [P, S], F32, 2)
-            nc.vector.scalar_tensor_tensor(diff[:], d3[:], -0.5, larger[t][:], ALU.mult, ALU.add)
-            nc.vector.tensor_scalar(z2[:, t, :], diff[:], gs_t[:, t : t + 1], None, ALU.mult)
+        b = [sb(f"b{t}", [P, S], F32) for t in range(PACK)]
+        larger = {}
+        diff = sb("diff", [P, PACK, S], F32)
         z2w = sb("z2w", [P, S], U32)
         z2s = sb("z2s", [P, S], U8)
-        quantise("z2q", z2[:], S, z2w[:], z2s[:])
-
-        members(2)
-
-        sig_bias = sb("sig_bias", [P, PACK], F32)
-        nc.vector.scalar_tensor_tensor(sig_bias[:], sl_t[:], -1.0, th_t[:], ALU.mult, ALU.mult)
-        b = [sb(f"b{t}", [P, S], F32) for t in range(PACK)]
-        b_again = [sb(f"b_again{t}", [P, S], F32) for t in range(PACK)]
-        for t in range(PACK):
-            product(banks[t][:], xc_w, xc_s, 0, t, z2w[:], z2s[:])
-            nc.scalar.activation(b[t][:], banks[t][:], ACT.Copy, scale=0.0625)
-            nc.sync.dma_start(b_again[t][:], b[t][:])
         sg = [sb(f"sg{h}", [P, PACK, HALF], F32) for h in range(2)]
-        step = [sb(f"step{h}", [P, PACK, HALF], F32) for h in range(2)]
-        for h, (cols, lst) in enumerate(halves(n4_l)):
-            for t in range(PACK):
-                nc.scalar.activation(sg[h][:, t, :], b[t][:].indirect(lst), ACT.Sigmoid, bias=sig_bias[:, t : t + 1], scale=sl_t[:, t : t + 1])
-        for h, (cols, lst) in enumerate(halves(n5_l)):
-            for t in range(PACK):
-                nc.vector.tensor_tensor(step[h][:, t, :], b[t][:].indirect(lst), b_again[t][:, cols], ALU.subtract)
-
+        step = {}
         ow = sb("ow", [P, S], U32)
         osc = sb("osc", [P, S], U8)
         out_rows = out_0.rearrange("(p t) j -> p t j", t=PACK)
         out_words = out_1[0].rearrange("p n t -> p (n t)").bitcast(I32)
+        sig_bias = sb("sig_bias", [P, PACK], F32)
+        b_again = sb("b_again", [P, PACK, S], F32)
 
-        def finish(c):
+        def exps():
+            larger_all = reuse("larger", "larger", [P, PACK, S], F32)
+            for t in range(PACK):
+                ea = ring("ea", [P, S], F32, 4)
+                for cols, lst in halves(n2_l):
+                    nc.scalar.activation(ea[:, cols], d[t][:].indirect(lst), ACT.Exp, bias=exp_bias[:, t : t + 1], scale=tau_t[:, t : t + 1])
+                larger[t] = larger_all[:, t, :]
+                nc.vector.scalar_tensor_tensor(larger[t], ea[:], 2.0, d[t][:], ALU.mult, ALU.max)
+
+        def diffs():
+            for t in range(PACK):
+                d3 = ring("d3", [P, S], F32, 4)
+                for cols, lst in halves(n3_l):
+                    if t in ():
+                        nc.vector.tensor_copy(d3[:, cols], d[t][:].indirect(lst))
+                    else:
+                        nc.scalar.activation(d3[:, cols], d[t][:].indirect(lst), ACT.Copy)
+                nc.vector.scalar_tensor_tensor(diff[:, t, :], d3[:], -0.5, larger[t], ALU.mult, ALU.add)
+            quantise_scaled("z2q", diff[:], gs_t, S, z2w[:], z2s[:])
+
+        def scores():
+            nc.vector.scalar_tensor_tensor(sig_bias[:], sl_t[:], -1.0, th_t[:], ALU.mult, ALU.mult)
+            for t in range(PACK):
+                product(banks[t][:], xc_w, xc_s, 0, t, z2w[:], z2s[:])
+                nc.scalar.activation(b[t][:], banks[t][:], ACT.Copy, scale=0.0625)
+                nc.sync.dma_start(b_again[:, t, :], b[t][:])
+
+        def gates(h):
+            cols, lst = halves(n4_l)[h]
+            for t in range(PACK):
+                nc.scalar.activation(sg[h][:, t, :], b[t][:].indirect(lst), ACT.Sigmoid, bias=sig_bias[:, t : t + 1], scale=sl_t[:, t : t + 1])
+
+        def steps_v(h):
+            cols, lst = halves(n5_l)[h]
+            step[h] = reuse("mbA", "step0", [P, PACK, HALF], F32)
+            for t in range(PACK):
+                nc.vector.tensor_tensor(step[h][:, t, :], b[t][:].indirect(lst), b_again[:, t, cols], ALU.subtract)
+
+        def steps_s(h):
+            cols, lst = halves(n5_l)[h]
+            b5 = sb(f"b5_{h}", [P, PACK, HALF], F32)
+            for t in range(PACK):
+                nc.scalar.activation(b5[:, t, :], b[t][:].indirect(lst), ACT.Copy)
+            step[h] = reuse(f"step{h}", "step1", [P, PACK, HALF], F32)
+            nc.vector.tensor_tensor(step[h][:], b5[:], b_again[:, :, cols], ALU.subtract)
+
+        def finish(c, weave):
             cols = slice(c * CHUNK, (c + 1) * CHUNK)
             h, part = divmod(c, 2)
             part_cols = slice(part * CHUNK, (part + 1) * CHUNK)
@@ -236,14 +259,38 @@ def tile_picked_tfcdmxbgspanecl_none_po_kernel(
             res = sb(f"res{c}", [P, PACK, CHUNK], F32)
             nc.vector.tensor_tensor(res[:], gated[:], step[h][:, :, part_cols], ALU.max)
             nc.sync.dma_start(out_rows[:, :, cols], res[:])
-            quantise(f"oq{c}", res[:], CHUNK, ow[:, cols], osc[:, cols])
+            woven = sb(f"oq{c}", [P, CHUNK, PACK], BF16)
+            weave(woven[:], res[:].rearrange("p t j -> p j t"))
+            nc.vector.quantize_mx(out=ow[:, cols].bitcast(FP8X4), scales=osc[:, cols], in_=woven[:].rearrange("p j t -> p (j t)"))
             nc.sync.dma_start(out_words[:, cols], ow[:, cols].bitcast(I32))
 
-        finish(0)
-        finish(1)
-        members(3)
-        finish(2)
-        finish(3)
+        xc_w0, xc_s0 = pick("xc", cand_l, ("top", "xc_scales"))
+        xc_w = deal(nc.vector.tensor_copy, "xc_w", xc_w0, U32, 4)
+        xc_s = deal(nc.vector.tensor_copy, "xc_s", xc_s0, U8, 16)
+        mb0 = fetch(0)
+        z0 = members(0, mb0)
+        exps()
+        diffs()
+        mb1 = fetch(1)
+        z1 = members(1, mb1)
+        mb2 = fetch(2)
+        scores()
+        z2 = members(2, mb2)
+        mb3 = fetch(3)
+        w3w = deal(nc.scalar.copy, "w3w", w3w_raw, U32, 4)
+        mix(0, *z0)
+        mix(1, *z1)
+        mix(2, *z2)
+        steps_v(0)
+        z3 = members(3, mb3)
+        mix(3, *z3)
+        gates(0)
+        finish(0, nc.vector.tensor_copy)
+        finish(1, nc.vector.tensor_copy)
+        gates(1)
+        steps_s(1)
+        finish(2, nc.vector.tensor_copy)
+        finish(3, nc.vector.tensor_copy)
         for q in range(4):
             queue = nc.scalar if q % 2 else nc.sync
             queue.dma_start(out_2[0, 4 * q : 4 * q + 4, :].bitcast(I32), osc[32 * q : 32 * q + 4, :].bitcast(I32))

@@ -99,17 +99,17 @@ def tile_picked_tfcdmxbgspanecl_none_po_kernel(
         xs = sb("xs", [P, T], U8)
         w1s_raw = sb("w1s_raw", [P, S], U8)
         w23s_raw = sb("w23s_raw", [P, S], U8)
-        nc.vector.memset(xs[:].bitcast(I32), 0)
-        nc.gpsimd.memset(w1s_raw[:].bitcast(I32), 0)
-        nc.gpsimd.memset(w23s_raw[:].bitcast(I32), 0)
+        nc.gpsimd.memset(xs[:].bitcast(I32), 0)
+        nc.vector.memset(w1s_raw[:].bitcast(I32), 0)
+        nc.vector.memset(w23s_raw[:].bitcast(I32), 0)
         y = [sb(f"y{t}", [P, S + SPARE], F32) for t in range(PACK)]
         for t in range(PACK):
             nc.gpsimd.memset(y[t][:, S:], 0.0)
 
-        xw = load_words("xw", x_words, T)
-        w1w_raw = load_words("w1w_raw", w1_words, S)
         offs_l = load_list("offs_l", offs)
+        xw = load_words("xw", x_words, T)
         load_scale_rows(nc.sync, xs, x_scales, 0)
+        w1w_raw = load_words("w1w_raw", w1_words, S)
         load_scale_rows(nc.sync, w1s_raw, w1_scales, 0)
         two_l = load_list("two_l", two)
         n1_l = load_list("n1_l", n1)
@@ -136,7 +136,7 @@ def tile_picked_tfcdmxbgspanecl_none_po_kernel(
             scaled = reuse(name + "_planes", name + "_planes", [P, PACK, width], BF16)
             for t in range(PACK):
                 nc.vector.tensor_scalar(scaled[:, t, :], planes[:, t, :], gain[:, t : t + 1], None, ALU.mult)
-            nc.vector.tensor_copy(woven[:], scaled[:].rearrange("p t j -> p j t"))
+            nc.vector.tensor_copy(woven[:].rearrange("p (m i) t -> p m t i", i=4), scaled[:].rearrange("p t (m i) -> p m t i", i=4))
             nc.vector.quantize_mx(out=words.bitcast(FP8X4), scales=scales, in_=woven[:].rearrange("p j t -> p (j t)"))
 
         w1s = deal(nc.vector.tensor_copy, "w1s", w1s_raw, U8, 16)
@@ -195,7 +195,7 @@ def tile_picked_tfcdmxbgspanecl_none_po_kernel(
         diff = sb("diff", [P, PACK, S], F32)
         z2w = sb("z2w", [P, S], U32)
         z2s = sb("z2s", [P, S], U8)
-        sg = [sb(f"sg{h}", [P, PACK, HALF], F32) for h in range(2)]
+        sg = [sb(f"sg{c}", [P, PACK, CHUNK], F32) for c in range(CHUNKS)]
         step = {}
         ow = sb("ow", [P, S], U32)
         osc = sb("osc", [P, S], U8)
@@ -205,7 +205,7 @@ def tile_picked_tfcdmxbgspanecl_none_po_kernel(
         b_again = sb("b_again", [P, PACK, S], F32)
 
         def exps():
-            larger_all = reuse("larger", "larger", [P, PACK, S], F32)
+            larger_all = reuse("mx", "larger", [P, PACK, S], F32)
             for t in range(PACK):
                 ea = ring("ea", [P, S], F32, 4)
                 for cols, lst in halves(n2_l):
@@ -231,10 +231,10 @@ def tile_picked_tfcdmxbgspanecl_none_po_kernel(
                 nc.scalar.activation(b[t][:], banks[t][:], ACT.Copy, scale=0.0625)
                 nc.sync.dma_start(b_again[:, t, :], b[t][:])
 
-        def gates(h):
-            cols, lst = halves(n4_l)[h]
+        def gates(c):
+            per = CHUNK // PER_COL
             for t in range(PACK):
-                nc.scalar.activation(sg[h][:, t, :], b[t][:].indirect(lst), ACT.Sigmoid, bias=sig_bias[:, t : t + 1], scale=sl_t[:, t : t + 1])
+                nc.scalar.activation(sg[c][:, t, :], b[t][:].indirect(n4_l[:, c * per : (c + 1) * per]), ACT.Sigmoid, bias=sig_bias[:, t : t + 1], scale=sl_t[:, t : t + 1])
 
         def steps_v(h):
             cols, lst = halves(n5_l)[h]
@@ -255,12 +255,12 @@ def tile_picked_tfcdmxbgspanecl_none_po_kernel(
             h, part = divmod(c, 2)
             part_cols = slice(part * CHUNK, (part + 1) * CHUNK)
             gated = ring("gated", [P, PACK, CHUNK], F32, 2)
-            nc.vector.tensor_tensor(gated[:], banks[4 + c][:].rearrange("p (t j) -> p t j", t=PACK), sg[h][:, :, part_cols], ALU.mult)
+            nc.vector.tensor_tensor(gated[:], banks[4 + c][:].rearrange("p (t j) -> p t j", t=PACK), sg[c][:], ALU.mult)
             res = sb(f"res{c}", [P, PACK, CHUNK], F32)
             nc.vector.tensor_tensor(res[:], gated[:], step[h][:, :, part_cols], ALU.max)
             nc.sync.dma_start(out_rows[:, :, cols], res[:])
             woven = sb(f"oq{c}", [P, CHUNK, PACK], BF16)
-            weave(woven[:], res[:].rearrange("p t j -> p j t"))
+            weave(woven[:].rearrange("p (m i) t -> p m t i", i=4), res[:].rearrange("p t (m i) -> p m t i", i=4))
             nc.vector.quantize_mx(out=ow[:, cols].bitcast(FP8X4), scales=osc[:, cols], in_=woven[:].rearrange("p j t -> p (j t)"))
             nc.sync.dma_start(out_words[:, cols], ow[:, cols].bitcast(I32))
 
@@ -286,10 +286,12 @@ def tile_picked_tfcdmxbgspanecl_none_po_kernel(
         mix(3, *z3)
         gates(0)
         finish(0, nc.vector.tensor_copy)
-        finish(1, nc.vector.tensor_copy)
         gates(1)
+        finish(1, nc.scalar.copy)
         steps_s(1)
-        finish(2, nc.vector.tensor_copy)
+        gates(2)
+        finish(2, nc.scalar.copy)
+        gates(3)
         finish(3, nc.vector.tensor_copy)
         for q in range(4):
             queue = nc.scalar if q % 2 else nc.sync

@@ -133,10 +133,12 @@ def tile_picked_tfcdmxbgspanecl_none_po_kernel(
 
         def quantise_scaled(name, planes, gain, width, words, scales):
             woven = reuse(name, name, [P, width, PACK], BF16)
-            scaled = reuse(name + "_planes", name + "_planes", [P, PACK, width], BF16)
-            for t in range(PACK):
-                nc.vector.tensor_scalar(scaled[:, t, :], planes[:, t, :], gain[:, t : t + 1], None, ALU.mult)
-            nc.vector.tensor_copy(woven[:].rearrange("p (m i) t -> p m t i", i=4), scaled[:].rearrange("p t (m i) -> p m t i", i=4))
+            nc.vector.tensor_tensor(
+                woven[:].rearrange("p (m e) t -> p m t e", e=2),
+                planes.rearrange("p t (m e) -> p m t e", e=2),
+                gain[:].unsqueeze(1).unsqueeze(3).to_broadcast([P, width // 2, PACK, 2]),
+                ALU.mult,
+            )
             nc.vector.quantize_mx(out=words.bitcast(FP8X4), scales=scales, in_=woven[:].rearrange("p j t -> p (j t)"))
 
         w1s = deal(nc.vector.tensor_copy, "w1s", w1s_raw, U8, 16)
@@ -192,7 +194,7 @@ def tile_picked_tfcdmxbgspanecl_none_po_kernel(
 
         b = [sb(f"b{t}", [P, S], F32) for t in range(PACK)]
         larger = {}
-        diff = sb("diff", [P, PACK, S], F32)
+        diff = reuse("z2q_planes", "diff", [P, PACK, S], F32)
         z2w = sb("z2w", [P, S], U32)
         z2s = sb("z2s", [P, S], U8)
         sg = [sb(f"sg{c}", [P, PACK, CHUNK], F32) for c in range(CHUNKS)]

@@ -14,6 +14,7 @@ ACT = mybir.ActivationFunctionType
 
 P = 128
 PACK = 4
+QUADRANTS = 4
 T = 2048
 S = 512
 MEMBERS = 4
@@ -22,7 +23,10 @@ CHUNKS = S // CHUNK
 HALF = S // 2
 SPARE = 32
 PER_COL = 16
-FLOPS = 4 * 2 * 512 * 512 * 512
+LINE = 16
+W3_ROW = 4
+SHARED_CHUNK = 1
+FLOPS = 4 * 2 * S * S * S
 
 
 def tile_picked_tfcdmxbgspanecl_none_po_kernel(
@@ -32,16 +36,16 @@ def tile_picked_tfcdmxbgspanecl_none_po_kernel(
     nc = tc.nc
     with ExitStack() as ctx:
         keep = ctx.enter_context(tc.tile_pool(name="keep", bufs=1))
-        work = ctx.enter_context(tc.tile_pool(name="work", bufs=2))
+        work = ctx.enter_context(tc.tile_pool(name="work", bufs=1))
         psum = ctx.enter_context(tc.psum_pool(name="psum", bufs=1))
 
-        def sb(name, shape, dtype):
+        def held(name, shape, dtype):
             return keep.tile(shape, dtype, name=name, align_bytes=64)
 
         def ring(tag, shape, dtype, bufs):
             return work.tile(shape, dtype, name=tag, tag=tag, bufs=bufs, align_bytes=64)
 
-        def reuse(tag, name, shape, dtype):
+        def shared(tag, name, shape, dtype):
             return work.tile(shape, dtype, name=name, tag=tag, bufs=1, align_bytes=64)
 
         def load_list(name, src):
@@ -50,37 +54,40 @@ def tile_picked_tfcdmxbgspanecl_none_po_kernel(
             return tile
 
         def load_words(name, src, width):
-            tile = sb(name, [P, width], U32)
+            tile = held(name, [P, width], U32)
             nc.sync.dma_start(tile[:].bitcast(I32), src[0].rearrange("p n t -> p (n t)").bitcast(I32))
             return tile
 
-        def load_scale_rows(queue, tile, src, first):
-            for q in range(4):
-                queue.dma_start(
+        def load_scale_rows(tile, src, first):
+            for q in range(QUADRANTS):
+                nc.sync.dma_start(
                     tile[32 * q + first : 32 * q + first + 4, :].bitcast(I32),
                     src[0, 4 * q : 4 * q + 4, :].bitcast(I32),
                 )
 
         def load_rows(name, src):
-            tile = reuse(name, name, [P, PACK], F32)
+            tile = shared(name, name, [P, PACK], F32)
             nc.sync.dma_start(tile[:], src.rearrange("(p t) o -> p (t o)", t=PACK))
             return tile
 
-        def deal(copy, name, src, dtype, run):
-            dst = sb(name, [P, S], dtype)
+        def deal(copy, tag, name, src, dtype, per_line):
+            dst = shared(tag, name, [P, S], dtype)
             copy(
-                dst[:].rearrange("p (t m i) -> p m t i", t=PACK, i=run),
-                src[:].rearrange("p (m i t) -> p m t i", t=PACK, i=run),
+                dst[:].rearrange("p (t m i) -> p m t i", t=PACK, i=per_line),
+                src[:].rearrange("p (m i t) -> p m t i", t=PACK, i=per_line),
             )
             return dst
 
-        def pick(name, lst, tags=None):
-            tags = tags or (name + "_words", name + "_scales")
-            words = reuse(tags[0], name + "_words", [P, S], U32)
-            scales = reuse(tags[1], name + "_scales", [P, S], U8)
-            nc.vector.tensor_copy(words[:], xw[:].indirect(lst[:]))
-            nc.vector.tensor_copy(scales[:], xs[:].indirect(lst[:]))
-            return words, scales
+        def deal_words(copy, tag, name, src):
+            return deal(copy, tag, name, src, U32, LINE // 4)
+
+        def deal_scales(name, src):
+            return deal(nc.vector.tensor_copy, name, name, src, U8, LINE)
+
+        def pick(tag, name, window, lst, dtype):
+            picked = shared(tag, name, [P, S], dtype)
+            nc.vector.tensor_copy(picked[:], window[:].indirect(lst[:]))
+            return picked
 
         def product(out, lhs_words, lhs_scales, first, t, rhs_words, rhs_scales):
             cols = slice(t * P, (t + 1) * P)
@@ -89,33 +96,48 @@ def tile_picked_tfcdmxbgspanecl_none_po_kernel(
                 rhs=rhs_words.bitcast(FP8X4), rhs_scale=rhs_scales, start=True, stop=True,
             )
 
-        def quantise(name, planes, width, words, scales):
-            woven = sb(name, [P, width, PACK], BF16)
-            nc.vector.tensor_copy(woven[:], planes.rearrange("p t j -> p j t"))
+        def quantise(woven, words, scales):
             nc.vector.quantize_mx(out=words.bitcast(FP8X4), scales=scales, in_=woven[:].rearrange("p j t -> p (j t)"))
 
-        banks = [psum.tile([P, S], F32, name=f"bank{i}") for i in range(8)]
+        def scale_and_quantise(name, planes, gain, width, words, scales):
+            woven = shared(name, name, [P, width, PACK], BF16)
+            nc.vector.tensor_tensor(
+                woven[:].rearrange("p (m e) t -> p m t e", e=2),
+                planes.rearrange("p t (m e) -> p m t e", e=2),
+                gain[:].unsqueeze(1).unsqueeze(3).to_broadcast([P, width // 2, PACK, 2]),
+                ALU.mult,
+            )
+            quantise(woven, words, scales)
 
-        xs = sb("xs", [P, T], U8)
-        w1s_raw = sb("w1s_raw", [P, S], U8)
-        w23s_raw = sb("w23s_raw", [P, S], U8)
-        nc.gpsimd.memset(xs[:].bitcast(I32), 0)
+        def entries_of(lst, first, count):
+            return lst[:, first // PER_COL : (first + count) // PER_COL]
+
+        def halves(lst):
+            return [(slice(h * HALF, (h + 1) * HALF), entries_of(lst, h * HALF, HALF)) for h in range(2)]
+
+        banks = [psum.tile([P, S], F32, name=f"bank{i}") for i in range(2 * PACK)]
+
+        xs = held("xs", [P, T], U8)
+        w1s_raw = shared("after_w1_scales", "w1s_raw", [P, S], U8)
+        w23s_raw = held("w23s_raw", [P, S], U8)
+        nc.gpsimd.memset(xs[:, : T // 2].bitcast(I32), 0)
+        nc.vector.memset(xs[:, T // 2 :].bitcast(I32), 0)
         nc.vector.memset(w1s_raw[:].bitcast(I32), 0)
         nc.vector.memset(w23s_raw[:].bitcast(I32), 0)
-        y = [sb(f"y{t}", [P, S + SPARE], F32) for t in range(PACK)]
+        y = [held(f"y{t}", [P, S + SPARE], F32) for t in range(PACK)]
         for t in range(PACK):
             nc.gpsimd.memset(y[t][:, S:], 0.0)
 
         offs_l = load_list("offs_l", offs)
-        xw = load_words("xw", x_words, T)
-        load_scale_rows(nc.sync, xs, x_scales, 0)
-        w1w_raw = load_words("w1w_raw", w1_words, S)
-        load_scale_rows(nc.sync, w1s_raw, w1_scales, 0)
         two_l = load_list("two_l", two)
         n1_l = load_list("n1_l", n1)
+        load_scale_rows(xs, x_scales, 0)
+        xw = load_words("xw", x_words, T)
+        w1w_raw = load_words("w1w_raw", w1_words, S)
+        load_scale_rows(w1s_raw, w1_scales, 0)
         w2w_raw = load_words("w2w_raw", w2_words, S)
-        load_scale_rows(nc.sync, w23s_raw, w2_scales, 0)
-        load_scale_rows(nc.sync, w23s_raw, w3_scales, 4)
+        load_scale_rows(w23s_raw, w2_scales, 0)
+        load_scale_rows(w23s_raw, w3_scales, W3_ROW)
         tau_t = load_rows("tau_t", tau)
         n2_l = load_list("n2_l", n2)
         cand_l = load_list("cand_l", cand)
@@ -128,173 +150,152 @@ def tile_picked_tfcdmxbgspanecl_none_po_kernel(
         sl_t = load_rows("sl_t", sl)
         th_t = load_rows("th_t", th)
 
-        def halves(lst):
-            return [(slice(h * HALF, (h + 1) * HALF), lst[:, h * HALF // PER_COL : (h + 1) * HALF // PER_COL]) for h in range(2)]
-
-        def quantise_scaled(name, planes, gain, width, words, scales):
-            woven = reuse(name, name, [P, width, PACK], BF16)
-            nc.vector.tensor_tensor(
-                woven[:].rearrange("p (m e) t -> p m t e", e=2),
-                planes.rearrange("p t (m e) -> p m t e", e=2),
-                gain[:].unsqueeze(1).unsqueeze(3).to_broadcast([P, width // 2, PACK, 2]),
-                ALU.mult,
-            )
-            nc.vector.quantize_mx(out=words.bitcast(FP8X4), scales=scales, in_=woven[:].rearrange("p j t -> p (j t)"))
-
-        w1s = deal(nc.vector.tensor_copy, "w1s", w1s_raw, U8, 16)
-        w1w = deal(nc.scalar.copy, "w1w", w1w_raw, U32, 4)
-        w2w = deal(nc.scalar.copy, "w2w", w2w_raw, U32, 4)
-        xo_w, xo_s = pick("xo", offs_l)
+        offs_s = pick("offs_s", "offs_s", xs, offs_l, U8)
+        two_s = pick("two_s", "two_s", xs, two_l, U8)
+        offs_w = pick("offs_w", "offs_w", xw, offs_l, U32)
+        w1s = deal_scales("w1s", w1s_raw)
+        w1w = deal_words(nc.scalar.copy, "w1w", "w1w", w1w_raw)
+        w2w = deal_words(nc.scalar.copy, "w2w", "w2w", w2w_raw)
         for t in range(PACK):
-            product(banks[t][:], w1w, w1s, 0, t, xo_w[:], xo_s[:])
+            product(banks[t][:], w1w, w1s, 0, t, offs_w[:], offs_s[:])
             nc.scalar.copy(y[t][:, :S], banks[t][:])
 
-        xt_w, xt_s = pick("xt", two_l)
-        w23s = deal(nc.vector.tensor_copy, "w23s", w23s_raw, U8, 16)
-        d = [sb(f"d{t}", [P, S], F32) for t in range(PACK)]
-        top = reuse("top", "top", [P, PACK], F32)
-        exp_bias = sb("exp_bias", [P, PACK], F32)
+        two_w = pick("after_w1_scales", "two_w", xw, two_l, U32)
+        w23s = deal_scales("w23s", w23s_raw)
+        d = [held(f"d{t}", [P, S], F32) for t in range(PACK)]
+        top = shared("after_exp_bias", "top", [P, PACK], F32)
+        exp_bias = held("exp_bias", [P, PACK], F32)
         for t in range(PACK):
-            product(banks[4 + t][:], w2w, w23s, 0, t, xt_w[:], xt_s[:])
-            nc.vector.tensor_scalar(d[t][:], banks[4 + t][:], 1.0, None, ALU.mult, ALU.max, accum_out=top[:, t : t + 1])
+            product(banks[PACK + t][:], w2w, w23s, 0, t, two_w[:], two_s[:])
+            nc.vector.tensor_scalar(d[t][:], banks[PACK + t][:], 1.0, None, ALU.mult, ALU.max, accum_out=top[:, t : t + 1])
         nc.vector.scalar_tensor_tensor(exp_bias[:], top[:], -1.0, tau_t[:], ALU.mult, ALU.mult)
 
-        entries = CHUNK * MEMBERS
-
-        def fetch(c):
-            lst = n1_l[:, c * entries // PER_COL : (c + 1) * entries // PER_COL]
-            mb = reuse(("mbA", "xc_scales", "mbA", "z2q")[c], f"mb{c}", [P, PACK, entries], F32)
+        def fetch_members(c, tag):
+            count = CHUNK * MEMBERS
+            lst = entries_of(n1_l, c * count, count)
+            mb = shared(tag, f"mb{c}", [P, PACK, count], F32)
             for t in range(PACK):
-                if (c, t) in ((1, 0),):
+                if c == SHARED_CHUNK and t == 0:
                     nc.vector.tensor_copy(mb[:, t, :], y[t][:].indirect(lst))
                 else:
                     nc.scalar.activation(mb[:, t, :], y[t][:].indirect(lst), ACT.Copy)
             return mb
 
-        def members(c, mb):
+        def make_z(c, mb, tag):
             four = mb[:].rearrange("p t (j e) -> p (t j) e", e=MEMBERS)
-            pairs = reuse(("top", "z2q_planes", "z2q_planes", "z2q_planes")[c], f"pairs{c}", [P, 2, PACK * CHUNK, 2], F32)
+            pairs = shared(tag, f"pairs{c}", [P, 2, PACK * CHUNK, 2], F32)
             hi, lo = pairs[:, 0], pairs[:, 1]
             nc.vector.tensor_tensor(hi, four[:, :, 0:2], four[:, :, 2:4], ALU.max)
             nc.vector.tensor_tensor(lo, four[:, :, 0:2], four[:, :, 2:4], ALU.min)
-            mx = reuse("mx", f"mx{c}", [P, PACK * CHUNK], F32)
-            mn = reuse("mn", f"mn{c}", [P, PACK * CHUNK], F32)
+            mx = shared("after_spread", f"mx{c}", [P, PACK * CHUNK], F32)
+            mn = shared("mn", f"mn{c}", [P, PACK * CHUNK], F32)
             nc.vector.tensor_tensor(mx[:], hi[:, :, 0], hi[:, :, 1], ALU.max)
             nc.vector.tensor_tensor(mn[:], lo[:, :, 0], lo[:, :, 1], ALU.min)
             spread = ring("spread", [P, PACK, CHUNK], F32, 2)
             nc.vector.scalar_tensor_tensor(spread[:].rearrange("p t j -> p (t j)"), mn[:], -0.5, mx[:], ALU.mult, ALU.add)
-            zw = sb(f"zw{c}", [P, CHUNK], U32)
-            zs = sb(f"zs{c}", [P, CHUNK], U8)
-            quantise_scaled(f"zq{c}", spread[:], gn_t, CHUNK, zw[:], zs[:])
-            return zw, zs
+            z_w = held(f"z_w{c}", [P, CHUNK], U32)
+            z_s = held(f"z_s{c}", [P, CHUNK], U8)
+            scale_and_quantise(f"z_woven{c}", spread[:], gn_t, CHUNK, z_w[:], z_s[:])
+            return z_w, z_s
 
-        def mix(c, zw, zs):
+        def make_a(c, z_w, z_s):
             for t in range(PACK):
-                product(banks[4 + c][:, t * CHUNK : (t + 1) * CHUNK], w3w, w23s, 4, t, zw[:], zs[:])
+                product(banks[PACK + c][:, t * CHUNK : (t + 1) * CHUNK], w3w, w23s, W3_ROW, t, z_w[:], z_s[:])
 
-        b = [sb(f"b{t}", [P, S], F32) for t in range(PACK)]
-        larger = {}
-        diff = reuse("z2q_planes", "diff", [P, PACK, S], F32)
-        z2w = sb("z2w", [P, S], U32)
-        z2s = sb("z2s", [P, S], U8)
-        sg = [sb(f"sg{c}", [P, PACK, CHUNK], F32) for c in range(CHUNKS)]
-        step = {}
-        ow = sb("ow", [P, S], U32)
-        osc = sb("osc", [P, S], U8)
+        b = [held(f"b{t}", [P, S], F32) for t in range(PACK)]
+        diff = shared("after_z2_weave", "diff", [P, PACK, S], F32)
+        z2_w = shared("after_b_words", "z2_w", [P, S], U32)
+        z2_s = shared("after_b_scales", "z2_s", [P, S], U8)
+        sg = [held(f"sg{c}", [P, PACK, CHUNK], F32) for c in range(CHUNKS)]
+        out_w = held("out_w", [P, S], U32)
+        out_s = held("out_s", [P, S], U8)
         out_rows = out_0.rearrange("(p t) j -> p t j", t=PACK)
         out_words = out_1[0].rearrange("p n t -> p (n t)").bitcast(I32)
-        sig_bias = sb("sig_bias", [P, PACK], F32)
-        b_again = sb("b_again", [P, PACK, S], F32)
+        sig_bias = held("sig_bias", [P, PACK], F32)
+        b_again = held("b_again", [P, PACK, S], F32)
 
-        def exps():
-            larger_all = reuse("mx", "larger", [P, PACK, S], F32)
+        def make_z2():
+            larger = shared("after_spread", "larger", [P, PACK, S], F32)
             for t in range(PACK):
-                ea = ring("ea", [P, S], F32, 4)
+                ea = ring("ea", [P, S], F32, PACK)
                 for cols, lst in halves(n2_l):
-                    nc.scalar.activation(ea[:, cols], d[t][:].indirect(lst), ACT.Exp, bias=exp_bias[:, t : t + 1], scale=tau_t[:, t : t + 1])
-                larger[t] = larger_all[:, t, :]
-                nc.vector.scalar_tensor_tensor(larger[t], ea[:], 2.0, d[t][:], ALU.mult, ALU.max)
-
-        def diffs():
+                    nc.scalar.activation(
+                        ea[:, cols], d[t][:].indirect(lst), ACT.Exp, bias=exp_bias[:, t : t + 1], scale=tau_t[:, t : t + 1]
+                    )
+                nc.vector.scalar_tensor_tensor(larger[:, t, :], ea[:], 2.0, d[t][:], ALU.mult, ALU.max)
             for t in range(PACK):
-                d3 = ring("d3", [P, S], F32, 4)
+                d3 = ring("d3", [P, S], F32, PACK)
                 for cols, lst in halves(n3_l):
-                    if t in ():
-                        nc.vector.tensor_copy(d3[:, cols], d[t][:].indirect(lst))
-                    else:
-                        nc.scalar.activation(d3[:, cols], d[t][:].indirect(lst), ACT.Copy)
-                nc.vector.scalar_tensor_tensor(diff[:, t, :], d3[:], -0.5, larger[t], ALU.mult, ALU.add)
-            quantise_scaled("z2q", diff[:], gs_t, S, z2w[:], z2s[:])
+                    nc.scalar.activation(d3[:, cols], d[t][:].indirect(lst), ACT.Copy)
+                nc.vector.scalar_tensor_tensor(diff[:, t, :], d3[:], -0.5, larger[:, t, :], ALU.mult, ALU.add)
+            scale_and_quantise("z2_woven", diff[:], gs_t, S, z2_w[:], z2_s[:])
 
-        def scores():
+        def make_b():
             nc.vector.scalar_tensor_tensor(sig_bias[:], sl_t[:], -1.0, th_t[:], ALU.mult, ALU.mult)
             for t in range(PACK):
-                product(banks[t][:], xc_w, xc_s, 0, t, z2w[:], z2s[:])
+                product(banks[t][:], cand_w, cand_s, 0, t, z2_w[:], z2_s[:])
                 nc.scalar.activation(b[t][:], banks[t][:], ACT.Copy, scale=0.0625)
                 nc.sync.dma_start(b_again[:, t, :], b[t][:])
 
-        def gates(c):
-            per = CHUNK // PER_COL
+        def make_sg(c):
+            lst = entries_of(n4_l, c * CHUNK, CHUNK)
             for t in range(PACK):
-                nc.scalar.activation(sg[c][:, t, :], b[t][:].indirect(n4_l[:, c * per : (c + 1) * per]), ACT.Sigmoid, bias=sig_bias[:, t : t + 1], scale=sl_t[:, t : t + 1])
+                nc.scalar.activation(
+                    sg[c][:, t, :], b[t][:].indirect(lst), ACT.Sigmoid, bias=sig_bias[:, t : t + 1], scale=sl_t[:, t : t + 1]
+                )
 
-        def steps_v(h):
-            cols, lst = halves(n5_l)[h]
-            step[h] = reuse("mbA", "step0", [P, PACK, HALF], F32)
-            for t in range(PACK):
-                nc.vector.tensor_tensor(step[h][:, t, :], b[t][:].indirect(lst), b_again[:, t, cols], ALU.subtract)
-
-        def steps_s(h):
-            cols, lst = halves(n5_l)[h]
-            b5 = sb(f"b5_{h}", [P, PACK, HALF], F32)
-            for t in range(PACK):
-                nc.scalar.activation(b5[:, t, :], b[t][:].indirect(lst), ACT.Copy)
-            step[h] = reuse(f"step{h}", "step1", [P, PACK, HALF], F32)
-            nc.vector.tensor_tensor(step[h][:], b5[:], b_again[:, :, cols], ALU.subtract)
-
-        def finish(c, weave):
+        def finish(c, step, weave):
             cols = slice(c * CHUNK, (c + 1) * CHUNK)
-            h, part = divmod(c, 2)
-            part_cols = slice(part * CHUNK, (part + 1) * CHUNK)
+            in_half = c * CHUNK % HALF
             gated = ring("gated", [P, PACK, CHUNK], F32, 2)
-            nc.vector.tensor_tensor(gated[:], banks[4 + c][:].rearrange("p (t j) -> p t j", t=PACK), sg[c][:], ALU.mult)
-            res = sb(f"res{c}", [P, PACK, CHUNK], F32)
-            nc.vector.tensor_tensor(res[:], gated[:], step[h][:, :, part_cols], ALU.max)
+            nc.vector.tensor_tensor(gated[:], banks[PACK + c][:].rearrange("p (t j) -> p t j", t=PACK), sg[c][:], ALU.mult)
+            res = held(f"res{c}", [P, PACK, CHUNK], F32)
+            nc.vector.tensor_tensor(res[:], gated[:], step[:, :, in_half : in_half + CHUNK], ALU.max)
             nc.sync.dma_start(out_rows[:, :, cols], res[:])
-            woven = sb(f"oq{c}", [P, CHUNK, PACK], BF16)
-            weave(woven[:].rearrange("p (m i) t -> p m t i", i=4), res[:].rearrange("p t (m i) -> p m t i", i=4))
-            nc.vector.quantize_mx(out=ow[:, cols].bitcast(FP8X4), scales=osc[:, cols], in_=woven[:].rearrange("p j t -> p (j t)"))
-            nc.sync.dma_start(out_words[:, cols], ow[:, cols].bitcast(I32))
+            woven = held(f"out_woven{c}", [P, CHUNK, PACK], BF16)
+            weave(
+                woven[:].rearrange("p (m i) t -> p m t i", i=LINE // 4),
+                res[:].rearrange("p t (m i) -> p m t i", i=LINE // 4),
+            )
+            quantise(woven, out_w[:, cols], out_s[:, cols])
+            nc.sync.dma_start(out_words[:, cols], out_w[:, cols].bitcast(I32))
 
-        xc_w0, xc_s0 = pick("xc", cand_l, ("top", "xc_scales"))
-        xc_w = deal(nc.vector.tensor_copy, "xc_w", xc_w0, U32, 4)
-        xc_s = deal(nc.vector.tensor_copy, "xc_s", xc_s0, U8, 16)
-        mb0 = fetch(0)
-        z0 = members(0, mb0)
-        exps()
-        diffs()
-        mb1 = fetch(1)
-        z1 = members(1, mb1)
-        mb2 = fetch(2)
-        scores()
-        z2 = members(2, mb2)
-        mb3 = fetch(3)
-        w3w = deal(nc.scalar.copy, "w3w", w3w_raw, U32, 4)
-        mix(0, *z0)
-        mix(1, *z1)
-        mix(2, *z2)
-        steps_v(0)
-        z3 = members(3, mb3)
-        mix(3, *z3)
-        gates(0)
-        finish(0, nc.vector.tensor_copy)
-        gates(1)
-        finish(1, nc.scalar.copy)
-        steps_s(1)
-        gates(2)
-        finish(2, nc.scalar.copy)
-        gates(3)
-        finish(3, nc.vector.tensor_copy)
-        for q in range(4):
+        cand_w_raw = pick("after_exp_bias", "cand_w_raw", xw, cand_l, U32)
+        cand_s_raw = pick("after_cand_scales", "cand_s_raw", xs, cand_l, U8)
+        cand_w = deal_words(nc.vector.tensor_copy, "cand_w", "cand_w", cand_w_raw)
+        cand_s = deal_scales("cand_s", cand_s_raw)
+
+        z_0 = make_z(0, fetch_members(0, "after_pairs"), "after_exp_bias")
+        make_z2()
+        z_1 = make_z(1, fetch_members(1, "after_cand_scales"), "after_z2_weave")
+        mb_2 = fetch_members(2, "after_pairs")
+        make_b()
+        z_2 = make_z(2, mb_2, "after_z2_weave")
+        mb_3 = fetch_members(3, "after_b_scales")
+        w3w = deal_words(nc.scalar.copy, "after_b_words", "w3w", w3w_raw)
+        for c, z_c in enumerate((z_0, z_1, z_2)):
+            make_a(c, *z_c)
+
+        (cols_0, n5_0), (cols_1, n5_1) = halves(n5_l)
+        step_0 = shared("after_pairs", "step_0", [P, PACK, HALF], F32)
+        for t in range(PACK):
+            nc.vector.tensor_tensor(step_0[:, t, :], b[t][:].indirect(n5_0), b_again[:, t, cols_0], ALU.subtract)
+        make_a(3, *make_z(3, mb_3, "after_z2_weave"))
+
+        make_sg(0)
+        finish(0, step_0, nc.vector.tensor_copy)
+        make_sg(1)
+        finish(1, step_0, nc.scalar.copy)
+        b5 = held("b5", [P, PACK, HALF], F32)
+        for t in range(PACK):
+            nc.scalar.activation(b5[:, t, :], b[t][:].indirect(n5_1), ACT.Copy)
+        step_1 = shared("step_1", "step_1", [P, PACK, HALF], F32)
+        nc.vector.tensor_tensor(step_1[:], b5[:], b_again[:, :, cols_1], ALU.subtract)
+        make_sg(2)
+        finish(2, step_1, nc.scalar.copy)
+        make_sg(3)
+        finish(3, step_1, nc.vector.tensor_copy)
+
+        for q in range(QUADRANTS):
             queue = nc.scalar if q % 2 else nc.sync
-            queue.dma_start(out_2[0, 4 * q : 4 * q + 4, :].bitcast(I32), osc[32 * q : 32 * q + 4, :].bitcast(I32))
+            queue.dma_start(out_2[0, 4 * q : 4 * q + 4, :].bitcast(I32), out_s[32 * q : 32 * q + 4, :].bitcast(I32))

from contextlib import ExitStack

import concourse.mybir as mybir

F32 = mybir.dt.float32
BF16 = mybir.dt.bfloat16
I32 = mybir.dt.int32
U32 = mybir.dt.uint32
U16 = mybir.dt.uint16
U8 = mybir.dt.uint8
FP8X4 = mybir.dt.float8_e4m3fn_x4
ALU = mybir.AluOpType
ACT = mybir.ActivationFunctionType

P = 128
PACK = 4
QUADRANTS = 4
T = 2048
S = 512
MEMBERS = 4
CHUNK = 128
CHUNKS = S // CHUNK
HALF = S // 2
SPARE = 32
PER_COL = 16
LINE = 16
W3_ROW = 4
SHARED_CHUNK = 1
FLOPS = 4 * 2 * S * S * S


def tile_picked_tfcdmxbgspanecl_none_po_kernel(
    tc, x_words, x_scales, w1_words, w1_scales, w2_words, w2_scales, tau, gn, w3_words, w3_scales,
    gs, sl, th, offs, two, n1, n2, n3, cand, n4, n5, out_0, out_1, out_2,
):
    nc = tc.nc
    with ExitStack() as ctx:
        keep = ctx.enter_context(tc.tile_pool(name="keep", bufs=1))
        work = ctx.enter_context(tc.tile_pool(name="work", bufs=1))
        psum = ctx.enter_context(tc.psum_pool(name="psum", bufs=1))

        def held(name, shape, dtype):
            return keep.tile(shape, dtype, name=name, align_bytes=64)

        def ring(tag, shape, dtype, bufs):
            return work.tile(shape, dtype, name=tag, tag=tag, bufs=bufs, align_bytes=64)

        def shared(tag, name, shape, dtype):
            return work.tile(shape, dtype, name=name, tag=tag, bufs=1, align_bytes=64)

        def load_list(name, src):
            tile = keep.tile(list(src.shape), U16, name=name)
            nc.sync.dma_start(tile[:], src)
            return tile

        def load_words(name, src, width):
            tile = held(name, [P, width], U32)
            nc.sync.dma_start(tile[:].bitcast(I32), src[0].rearrange("p n t -> p (n t)").bitcast(I32))
            return tile

        def load_scale_rows(tile, src, first):
            for q in range(QUADRANTS):
                nc.sync.dma_start(
                    tile[32 * q + first : 32 * q + first + 4, :].bitcast(I32),
                    src[0, 4 * q : 4 * q + 4, :].bitcast(I32),
                )

        def load_rows(name, src):
            tile = shared(name, name, [P, PACK], F32)
            nc.sync.dma_start(tile[:], src.rearrange("(p t) o -> p (t o)", t=PACK))
            return tile

        def deal(copy, tag, name, src, dtype, per_line):
            dst = shared(tag, name, [P, S], dtype)
            copy(
                dst[:].rearrange("p (t m i) -> p m t i", t=PACK, i=per_line),
                src[:].rearrange("p (m i t) -> p m t i", t=PACK, i=per_line),
            )
            return dst

        def deal_words(copy, tag, name, src):
            return deal(copy, tag, name, src, U32, LINE // 4)

        def deal_scales(name, src):
            return deal(nc.vector.tensor_copy, name, name, src, U8, LINE)

        def pick(tag, name, window, lst, dtype):
            picked = shared(tag, name, [P, S], dtype)
            nc.vector.tensor_copy(picked[:], window[:].indirect(lst[:]))
            return picked

        def product(out, lhs_words, lhs_scales, first, t, rhs_words, rhs_scales):
            cols = slice(t * P, (t + 1) * P)
            nc.tensor.matmul_mx(
                out=out, lhsT=lhs_words[:, cols].bitcast(FP8X4), lhsT_scale=lhs_scales[first:P, cols],
                rhs=rhs_words.bitcast(FP8X4), rhs_scale=rhs_scales, start=True, stop=True,
            )

        def quantise(woven, words, scales):
            nc.vector.quantize_mx(out=words.bitcast(FP8X4), scales=scales, in_=woven[:].rearrange("p j t -> p (j t)"))

        def scale_and_quantise(name, planes, gain, width, words, scales):
            woven = shared(name, name, [P, width, PACK], BF16)
            nc.vector.tensor_tensor(
                woven[:].rearrange("p (m e) t -> p m t e", e=2),
                planes.rearrange("p t (m e) -> p m t e", e=2),
                gain[:].unsqueeze(1).unsqueeze(3).to_broadcast([P, width // 2, PACK, 2]),
                ALU.mult,
            )
            quantise(woven, words, scales)

        def entries_of(lst, first, count):
            return lst[:, first // PER_COL : (first + count) // PER_COL]

        def halves(lst):
            return [(slice(h * HALF, (h + 1) * HALF), entries_of(lst, h * HALF, HALF)) for h in range(2)]

        banks = [psum.tile([P, S], F32, name=f"bank{i}") for i in range(2 * PACK)]

        xs = held("xs", [P, T], U8)
        w1s_raw = shared("after_w1_scales", "w1s_raw", [P, S], U8)
        w23s_raw = held("w23s_raw", [P, S], U8)
        nc.gpsimd.memset(xs[:, : T // 2].bitcast(I32), 0)
        nc.vector.memset(xs[:, T // 2 :].bitcast(I32), 0)
        nc.vector.memset(w1s_raw[:].bitcast(I32), 0)
        nc.vector.memset(w23s_raw[:].bitcast(I32), 0)
        y = [held(f"y{t}", [P, S + SPARE], F32) for t in range(PACK)]
        for t in range(PACK):
            nc.gpsimd.memset(y[t][:, S:], 0.0)

        offs_l = load_list("offs_l", offs)
        two_l = load_list("two_l", two)
        n1_l = load_list("n1_l", n1)
        load_scale_rows(xs, x_scales, 0)
        xw = load_words("xw", x_words, T)
        w1w_raw = load_words("w1w_raw", w1_words, S)
        load_scale_rows(w1s_raw, w1_scales, 0)
        w2w_raw = load_words("w2w_raw", w2_words, S)
        load_scale_rows(w23s_raw, w2_scales, 0)
        load_scale_rows(w23s_raw, w3_scales, W3_ROW)
        tau_t = load_rows("tau_t", tau)
        n2_l = load_list("n2_l", n2)
        cand_l = load_list("cand_l", cand)
        gn_t = load_rows("gn_t", gn)
        w3w_raw = load_words("w3w_raw", w3_words, S)
        n3_l = load_list("n3_l", n3)
        gs_t = load_rows("gs_t", gs)
        n4_l = load_list("n4_l", n4)
        n5_l = load_list("n5_l", n5)
        sl_t = load_rows("sl_t", sl)
        th_t = load_rows("th_t", th)

        offs_s = pick("offs_s", "offs_s", xs, offs_l, U8)
        two_s = pick("two_s", "two_s", xs, two_l, U8)
        offs_w = pick("offs_w", "offs_w", xw, offs_l, U32)
        w1s = deal_scales("w1s", w1s_raw)
        w1w = deal_words(nc.scalar.copy, "w1w", "w1w", w1w_raw)
        w2w = deal_words(nc.scalar.copy, "w2w", "w2w", w2w_raw)
        for t in range(PACK):
            product(banks[t][:], w1w, w1s, 0, t, offs_w[:], offs_s[:])
            nc.scalar.copy(y[t][:, :S], banks[t][:])

        two_w = pick("after_w1_scales", "two_w", xw, two_l, U32)
        w23s = deal_scales("w23s", w23s_raw)
        d = [held(f"d{t}", [P, S], F32) for t in range(PACK)]
        top = shared("after_exp_bias", "top", [P, PACK], F32)
        exp_bias = held("exp_bias", [P, PACK], F32)
        for t in range(PACK):
            product(banks[PACK + t][:], w2w, w23s, 0, t, two_w[:], two_s[:])
            nc.vector.tensor_scalar(d[t][:], banks[PACK + t][:], 1.0, None, ALU.mult, ALU.max, accum_out=top[:, t : t + 1])
        nc.vector.scalar_tensor_tensor(exp_bias[:], top[:], -1.0, tau_t[:], ALU.mult, ALU.mult)

        def fetch_members(c, tag):
            count = CHUNK * MEMBERS
            lst = entries_of(n1_l, c * count, count)
            mb = shared(tag, f"mb{c}", [P, PACK, count], F32)
            for t in range(PACK):
                if c == SHARED_CHUNK and t == 0:
                    nc.vector.tensor_copy(mb[:, t, :], y[t][:].indirect(lst))
                else:
                    nc.scalar.activation(mb[:, t, :], y[t][:].indirect(lst), ACT.Copy)
            return mb

        def make_z(c, mb, tag):
            four = mb[:].rearrange("p t (j e) -> p (t j) e", e=MEMBERS)
            pairs = shared(tag, f"pairs{c}", [P, 2, PACK * CHUNK, 2], F32)
            hi, lo = pairs[:, 0], pairs[:, 1]
            nc.vector.tensor_tensor(hi, four[:, :, 0:2], four[:, :, 2:4], ALU.max)
            nc.vector.tensor_tensor(lo, four[:, :, 0:2], four[:, :, 2:4], ALU.min)
            mx = shared("after_spread", f"mx{c}", [P, PACK * CHUNK], F32)
            mn = shared("mn", f"mn{c}", [P, PACK * CHUNK], F32)
            nc.vector.tensor_tensor(mx[:], hi[:, :, 0], hi[:, :, 1], ALU.max)
            nc.vector.tensor_tensor(mn[:], lo[:, :, 0], lo[:, :, 1], ALU.min)
            spread = ring("spread", [P, PACK, CHUNK], F32, 2)
            nc.vector.scalar_tensor_tensor(spread[:].rearrange("p t j -> p (t j)"), mn[:], -0.5, mx[:], ALU.mult, ALU.add)
            z_w = held(f"z_w{c}", [P, CHUNK], U32)
            z_s = held(f"z_s{c}", [P, CHUNK], U8)
            scale_and_quantise(f"z_woven{c}", spread[:], gn_t, CHUNK, z_w[:], z_s[:])
            return z_w, z_s

        def make_a(c, z_w, z_s):
            for t in range(PACK):
                product(banks[PACK + c][:, t * CHUNK : (t + 1) * CHUNK], w3w, w23s, W3_ROW, t, z_w[:], z_s[:])

        b = [held(f"b{t}", [P, S], F32) for t in range(PACK)]
        diff = shared("after_z2_weave", "diff", [P, PACK, S], F32)
        z2_w = shared("after_b_words", "z2_w", [P, S], U32)
        z2_s = shared("after_b_scales", "z2_s", [P, S], U8)
        sg = [held(f"sg{c}", [P, PACK, CHUNK], F32) for c in range(CHUNKS)]
        out_w = held("out_w", [P, S], U32)
        out_s = held("out_s", [P, S], U8)
        out_rows = out_0.rearrange("(p t) j -> p t j", t=PACK)
        out_words = out_1[0].rearrange("p n t -> p (n t)").bitcast(I32)
        sig_bias = held("sig_bias", [P, PACK], F32)
        b_again = held("b_again", [P, PACK, S], F32)

        def make_z2():
            larger = shared("after_spread", "larger", [P, PACK, S], F32)
            for t in range(PACK):
                ea = ring("ea", [P, S], F32, PACK)
                for cols, lst in halves(n2_l):
                    nc.scalar.activation(
                        ea[:, cols], d[t][:].indirect(lst), ACT.Exp, bias=exp_bias[:, t : t + 1], scale=tau_t[:, t : t + 1]
                    )
                nc.vector.scalar_tensor_tensor(larger[:, t, :], ea[:], 2.0, d[t][:], ALU.mult, ALU.max)
            for t in range(PACK):
                d3 = ring("d3", [P, S], F32, PACK)
                for cols, lst in halves(n3_l):
                    nc.scalar.activation(d3[:, cols], d[t][:].indirect(lst), ACT.Copy)
                nc.vector.scalar_tensor_tensor(diff[:, t, :], d3[:], -0.5, larger[:, t, :], ALU.mult, ALU.add)
            scale_and_quantise("z2_woven", diff[:], gs_t, S, z2_w[:], z2_s[:])

        def make_b():
            nc.vector.scalar_tensor_tensor(sig_bias[:], sl_t[:], -1.0, th_t[:], ALU.mult, ALU.mult)
            for t in range(PACK):
                product(banks[t][:], cand_w, cand_s, 0, t, z2_w[:], z2_s[:])
                nc.scalar.activation(b[t][:], banks[t][:], ACT.Copy, scale=0.0625)
                nc.sync.dma_start(b_again[:, t, :], b[t][:])

        def make_sg(c):
            lst = entries_of(n4_l, c * CHUNK, CHUNK)
            for t in range(PACK):
                nc.scalar.activation(
                    sg[c][:, t, :], b[t][:].indirect(lst), ACT.Sigmoid, bias=sig_bias[:, t : t + 1], scale=sl_t[:, t : t + 1]
                )

        def finish(c, step, weave):
            cols = slice(c * CHUNK, (c + 1) * CHUNK)
            in_half = c * CHUNK % HALF
            gated = ring("gated", [P, PACK, CHUNK], F32, 2)
            nc.vector.tensor_tensor(gated[:], banks[PACK + c][:].rearrange("p (t j) -> p t j", t=PACK), sg[c][:], ALU.mult)
            res = held(f"res{c}", [P, PACK, CHUNK], F32)
            nc.vector.tensor_tensor(res[:], gated[:], step[:, :, in_half : in_half + CHUNK], ALU.max)
            nc.sync.dma_start(out_rows[:, :, cols], res[:])
            woven = held(f"out_woven{c}", [P, CHUNK, PACK], BF16)
            weave(
                woven[:].rearrange("p (m i) t -> p m t i", i=LINE // 4),
                res[:].rearrange("p t (m i) -> p m t i", i=LINE // 4),
            )
            quantise(woven, out_w[:, cols], out_s[:, cols])
            nc.sync.dma_start(out_words[:, cols], out_w[:, cols].bitcast(I32))

        cand_w_raw = pick("after_exp_bias", "cand_w_raw", xw, cand_l, U32)
        cand_s_raw = pick("after_cand_scales", "cand_s_raw", xs, cand_l, U8)
        cand_w = deal_words(nc.vector.tensor_copy, "cand_w", "cand_w", cand_w_raw)
        cand_s = deal_scales("cand_s", cand_s_raw)

        z_0 = make_z(0, fetch_members(0, "after_pairs"), "after_exp_bias")
        make_z2()
        z_1 = make_z(1, fetch_members(1, "after_cand_scales"), "after_z2_weave")
        mb_2 = fetch_members(2, "after_pairs")
        make_b()
        z_2 = make_z(2, mb_2, "after_z2_weave")
        mb_3 = fetch_members(3, "after_b_scales")
        w3w = deal_words(nc.scalar.copy, "after_b_words", "w3w", w3w_raw)
        for c, z_c in enumerate((z_0, z_1, z_2)):
            make_a(c, *z_c)

        (cols_0, n5_0), (cols_1, n5_1) = halves(n5_l)
        step_0 = shared("after_pairs", "step_0", [P, PACK, HALF], F32)
        for t in range(PACK):
            nc.vector.tensor_tensor(step_0[:, t, :], b[t][:].indirect(n5_0), b_again[:, t, cols_0], ALU.subtract)
        make_a(3, *make_z(3, mb_3, "after_z2_weave"))

        make_sg(0)
        finish(0, step_0, nc.vector.tensor_copy)
        make_sg(1)
        finish(1, step_0, nc.scalar.copy)
        b5 = held("b5", [P, PACK, HALF], F32)
        for t in range(PACK):
            nc.scalar.activation(b5[:, t, :], b[t][:].indirect(n5_1), ACT.Copy)
        step_1 = shared("step_1", "step_1", [P, PACK, HALF], F32)
        nc.vector.tensor_tensor(step_1[:], b5[:], b_again[:, :, cols_1], ALU.subtract)
        make_sg(2)
        finish(2, step_1, nc.scalar.copy)
        make_sg(3)
        finish(3, step_1, nc.vector.tensor_copy)

        for q in range(QUADRANTS):
            queue = nc.scalar if q % 2 else nc.sync
            queue.dma_start(out_2[0, 4 * q : 4 * q + 4, :].bitcast(I32), out_s[32 * q : 32 * q + 4, :].bitcast(I32))
